import numpy as np
import ml_dtypes


def mxq(x, axis, fmt="e4m3"):
    dtype, down = {"e4m3": (ml_dtypes.float8_e4m3fn, 7), "e5m2": (ml_dtypes.float8_e5m2, 14)}[fmt]
    v = np.moveaxis(np.asarray(x, np.float32).astype(ml_dtypes.bfloat16).astype(np.float64), axis, -1)
    blocks = v.reshape(v.shape[:-1] + (-1, 32))
    amax = np.abs(blocks).max(-1, keepdims=True)
    byte = np.maximum(np.where(amax > 0, np.frexp(amax)[1] - 1 + 127, 0) - down, 1)
    scale = np.exp2(byte - 127.0)
    codes = (blocks / scale).astype(np.float32).astype(dtype).astype(np.float64)
    return np.moveaxis((codes * scale).reshape(v.shape), -1, axis)


WIDE = False


def mx_kscale(k):
    if not WIDE:
        return np.ones(k)
    levels = np.array([10, -10, 5, -5, 0])
    if k % 512:
        return np.exp2(np.random.permutation(np.resize(levels, k // 32))).repeat(32)
    a = np.empty((k // 512, 16))
    for p in range(k // 512):
        a[p, :8] = np.random.permutation(np.resize(levels, 8))
        for g in range(8):
            far = levels[np.abs(levels - a[p, g]) >= 10]
            a[p, g + 8] = far[np.random.randint(len(far))]
    return np.exp2(a.ravel()).repeat(32)


BF16 = ml_dtypes.bfloat16


def bf(x):
    return np.asarray(x, np.float32).astype(BF16)


def f64(x):
    return np.asarray(x).astype(np.float64)


E2M1 = np.array([0.0, 0.5, 1.0, 1.5, 2.0, 3.0, 4.0, 6.0, -0.0, -0.5, -1.0, -1.5, -2.0, -3.0, -4.0, -6.0])


def pack_weight(w, fmt):
    k, n = w.shape
    w = f64(bf(w)).reshape(k // 32, 32, n)
    amax = np.abs(w).max(1)
    if fmt == "e4m3":
        byte = np.frexp(amax)[1] - 1 + 127 - 7
    else:
        mant, ex = np.frexp(amax / 6.0)
        byte = np.where(mant > 0.5, ex, ex - 1) + 127
    byte = np.clip(np.where(amax > 0, byte, 1), 1, 254)
    scaled = (w * np.exp2(127.0 - byte)[:, None, :]).reshape(k, n).astype(np.float32)
    by_word = np.ascontiguousarray(scaled.reshape(k // 512, 128, 4, n).transpose(0, 1, 3, 2))
    if fmt == "e4m3":
        words = by_word.astype(ml_dtypes.float8_e4m3fn).view(np.uint8)
    else:
        c = by_word.astype(ml_dtypes.float4_e2m1fn).view(np.uint8) & 0xF
        words = c[..., 0::2] | (c[..., 1::2] << 4)
    return np.ascontiguousarray(words), np.ascontiguousarray(byte.astype(np.uint8).reshape(k // 512, 16, n))


def unpack_weight(words, scales, fmt):
    g, p, n, _ = words.shape
    if fmt == "e4m3":
        vals = np.ascontiguousarray(words).view(ml_dtypes.float8_e4m3fn).astype(np.float64)
    else:
        nib = np.empty((g, p, n, 4), np.uint8)
        nib[..., 0::2] = words & 0xF
        nib[..., 1::2] = words >> 4
        vals = E2M1[nib]
    vals = vals * np.repeat(np.exp2(scales.astype(np.float64) - 127.0), 8, axis=1)[..., None]
    return vals.transpose(0, 1, 3, 2).reshape(g * 512, n)
def pack4(w):
    words, scales = pack_weight(w, "e2m1")
    return words.reshape(words.shape[0], 128, -1), scales


def unpack4(words, scales):
    return unpack_weight(words.reshape(words.shape[0], 128, -1, 2), scales, "e2m1")


G, M, K, V, J = 3, 2048, 512, 1024, 128


def setup_inputs():
    s = mx_kscale(K)
    t = mx_kscale(G * V).reshape(G, V)
    shapes = np.random.standard_normal((G, K, V)) / np.sqrt(K) / s[:, None] * t[:, None, :]
    regressor = np.random.standard_normal((G, V, J)) / np.sqrt(V) / t[:, :, None]
    shape_words, shape_scales = pack4(shapes.reshape(G * K, V))
    reg_words, reg_scales = pack4(regressor.reshape(G * V, J))
    return {"betas": bf(np.random.standard_normal((M, K)) * s),
            "shape_words": shape_words,
            "shape_scales": shape_scales,
            "template": bf(0.5 * np.random.standard_normal((G, V)) * t),
            "stature": bf(1 + 0.1 * np.random.standard_normal(M)),
            "reg_words": reg_words,
            "reg_scales": reg_scales,
            "trans": bf(0.5 * np.random.standard_normal((M, G)))}


def reference(betas, shape_words, shape_scales, template, stature, reg_words, reg_scales, trans):
    b = mxq(f64(betas), 1, "e4m3")
    shapes = unpack4(shape_words, shape_scales)
    regressor = unpack4(reg_words, reg_scales)
    size = f64(stature)[:, None]
    mean = f64(template)
    shift = f64(trans)
    joints = []
    for c in range(G):
        offsets = b @ shapes[c * K:(c + 1) * K]
        verts = (offsets + mean[c]) * size
        rest = mxq(verts, 1, "e4m3") @ regressor[c * V:(c + 1) * V]
        joints.append(rest + shift[:, c:c + 1])
    return np.stack(joints)

@@ -1,0 +1,251 @@
+from contextlib import ExitStack
+
+import concourse.mybir as mybir
+from concourse.masks import make_identity
+
+F32 = mybir.dt.float32
+BF16 = mybir.dt.bfloat16
+I32 = mybir.dt.int32
+U32 = mybir.dt.uint32
+U8 = mybir.dt.uint8
+FP8X4 = mybir.dt.float8_e4m3fn_x4
+FP4X4 = mybir.dt.float4_e2m1fn_x4
+ADD = mybir.AluOpType.add
+MULT = mybir.AluOpType.mult
+IDENTITY = mybir.ActivationFunctionType.Identity
+
+G, M, K, V, J = 3, 2048, 512, 1024, 128
+FLOPS = 2 * G * M * V * (K + J)
+P = 128
+NP = 512
+BLOCKS = M // NP
+STEPS = BLOCKS * G
+V_PERSONS = 128
+G_CHUNK = 128
+
+
+def tile_body_model_joints_s14_kernel(
+    tc, betas, shape_words, shape_scales, template, stature, reg_words, reg_scales, trans, out
+):
+    nc = tc.nc
+    with ExitStack() as ctx:
+        keep = ctx.enter_context(tc.tile_pool(name="keep", bufs=1))
+        work = ctx.enter_context(tc.tile_pool(name="work", bufs=3))
+        banks = ctx.enter_context(tc.psum_pool(name="banks", bufs=6))
+        joint_banks = ctx.enter_context(tc.psum_pool(name="joint_banks", bufs=1))
+        size_banks = ctx.enter_context(tc.psum_pool(name="size_banks", bufs=1))
+        ctx.enter_context(tc.manual_schedule())
+
+        ident_f32 = keep.tile([P, P], F32, name="ident_f32")
+        ident_bf = keep.tile([P, P], BF16, name="ident_bf")
+        raw_words = [keep.tile([P, 2 * V], U8, name="raw_words%d" % c, align_bytes=64) for c in range(G)]
+        raw_scales = [keep.tile([P, V], U8, name="raw_scales%d" % c, align_bytes=64) for c in range(G)]
+        s_words = [[keep.tile([P, V], U8, name="s_words%d%d" % (c, h), align_bytes=64) for h in range(2)] for c in range(G)]
+        s_scales = [[keep.tile([P, V // 2], U8, name="s_scales%d%d" % (c, h), align_bytes=64) for h in range(2)] for c in range(G)]
+        r_words = keep.tile([P, 2 * G, 2 * J], U8, name="r_words", align_bytes=64)
+        r_scales = keep.tile([P, 2 * G, J], U8, name="r_scales", align_bytes=64)
+        mean_bf = keep.tile([P, 2 * G, 4], BF16, name="mean_bf")
+        mean = keep.tile([P, 2 * G, 4], F32, name="mean")
+        stat = keep.tile([P, BLOCKS, 4], BF16, name="stat")
+        shift = keep.tile([P, BLOCKS, 4 * G], BF16, name="shift")
+        dummy = keep.tile([P, 1], F32, name="dummy")
+        people = [keep.tile([P, 4, K], BF16, name="people%d" % b, align_bytes=64) for b in range(BLOCKS)]
+        size_ps = size_banks.tile([P, 2, NP], BF16, name="size_ps")
+
+        people_hbm = betas.rearrange("(b p i) k -> b p i k", p=P, i=4)
+        words_hbm = shape_words.bitcast(I32)
+        scales_hbm = shape_scales.bitcast(I32).rearrange("c (q r) n -> c r q n", r=4)
+        rwords_hbm = reg_words.bitcast(I32).rearrange("g p n -> p g n")
+        rscales_hbm = reg_scales.bitcast(I32).rearrange("g (q r) n -> r q g n", r=4)
+        mean_hbm = template.rearrange("c n -> (c n)").rearrange("(g p t) -> p g t", p=P, t=4)
+        out_hbm = out.rearrange("c (b p i) j -> c b p i j", p=P, i=4)
+
+        for c in range(G):
+            nc.vector.memset(raw_scales[c][:].bitcast(I32), 0)
+        nc.vector.memset(r_scales[:].rearrange("p g n -> p (g n)").bitcast(I32), 0)
+        nc.vector.memset(dummy[:], 0.0)
+        make_identity(nc, ident_f32[:])
+        make_identity(nc, ident_bf[:])
+
+        def load_words(c, h):
+            nc.sync.dma_start(
+                out=raw_words[c][:, h * V : (h + 1) * V].bitcast(I32), in_=words_hbm[c, :, h * 256 : (h + 1) * 256]
+            )
+
+        def load_scales(eng, c):
+            for r in range(4):
+                eng.dma_start(out=raw_scales[c][:].bitcast(I32)[r:P:32, :], in_=scales_hbm[c, r])
+
+        load_words(0, 0)
+        load_scales(nc.sync, 0)
+        for i in (0, 2):
+            nc.sync.dma_start(out=people[0][:, i : i + 2, :], in_=people_hbm[0, :, i : i + 2, :])
+        load_words(0, 1)
+        for c in (1, 2):
+            for h in range(2):
+                load_words(c, h)
+        nc.sync.dma_start(out=r_words[:].rearrange("p g n -> p (g n)").bitcast(I32).rearrange("p (g n) -> p g n", g=2 * G), in_=rwords_hbm)
+        for b in range(1, BLOCKS):
+            nc.sync.dma_start(out=people[b][:], in_=people_hbm[b])
+
+        nc.scalar.dma_start(out=stat[:], in_=stature.rearrange("(b p i) -> p b i", p=P, i=4))
+        nc.scalar.dma_start(out=mean_bf[:], in_=mean_hbm)
+        nc.scalar.activation(out=dummy[:], in_=dummy[:], func=IDENTITY)
+        load_scales(nc.scalar, 1)
+        load_scales(nc.scalar, 2)
+        for r in range(4):
+            nc.scalar.dma_start(
+                out=r_scales[:].rearrange("p g n -> p (g n)").bitcast(I32)[r:P:32, :].rearrange("p (g n) -> p g n", g=2 * G),
+                in_=rscales_hbm[r],
+            )
+        nc.scalar.dma_start(out=shift[:], in_=trans.rearrange("(b p i) c -> p b (i c)", p=P, i=4))
+
+        def permute(c, h):
+            nc.vector.tensor_copy(
+                out=s_words[c][h][:].rearrange("p (t m b) -> p t m b", t=4, b=2),
+                in_=raw_words[c][:, h * V : (h + 1) * V].rearrange("p (m t b) -> p t m b", t=4, b=2),
+            )
+            nc.vector.tensor_copy(
+                out=s_scales[c][h][:].rearrange("p (t m) -> p t m", t=4),
+                in_=raw_scales[c][:, h * 512 : (h + 1) * 512].rearrange("p (m t) -> p t m", t=4),
+            )
+
+        b_codes = {}
+        size_sb = {}
+        grouped = {}
+
+        def spread_sizes(b):
+            half = size_ps[:, b % 2, :]
+            for i in range(4):
+                nc.tensor.transpose(half[:, i * P : (i + 1) * P], stat[:, b, i : i + 1].to_broadcast([P, P]), ident_bf[:])
+            sb = work.tile([P, NP], BF16, name="size_sb", tag="size_sb", bufs=2)
+            nc.scalar.copy(out=sb[:], in_=half)
+            size_sb[b] = sb
+
+        def turn_people(b, engines):
+            words = people[b][:].rearrange("p i k -> p (i k)").bitcast(F32)
+            gr = work.tile([P, NP * 4], BF16, name="b_grouped", tag="b_grouped", bufs=2, align_bytes=64)
+            grouped[b] = gr
+            for pair in range(2):
+                bank = banks.tile([P, 2, 2, P], F32, name="bank_t", tag="bank")
+                for a in range(2):
+                    i = 2 * pair + a
+                    for u in range(2):
+                        nc.tensor.transpose(bank[:, a, u, :], words[:, 256 * i + u : 256 * (i + 1) : 2], ident_f32[:])
+                dst = gr[:, pair * 1024 : (pair + 1) * 1024].bitcast(F32).rearrange("p (a n u) -> p a n u", a=2, u=2)
+                src = bank[:].rearrange("p a u n -> p a n u")
+                if engines[pair] == "v":
+                    nc.vector.tensor_copy(out=dst, in_=src)
+                else:
+                    nc.scalar.copy(out=dst, in_=src)
+
+        def quantize_people(b):
+            codes = work.tile([P, NP], U32, name="b_codes", tag="b_codes", bufs=2, align_bytes=64)
+            scales = work.tile([P, NP], U8, name="b_scales", tag="b_scales", bufs=2, align_bytes=64)
+            nc.vector.quantize_mx(out=codes[:].bitcast(FP8X4), scales=scales[:], in_=grouped[b][:])
+            b_codes[b] = (codes, scales)
+
+        nc.vector.tensor_copy(out=mean[:], in_=mean_bf[:])
+        permute(0, 0)
+        spread_sizes(0)
+        turn_people(0, "sv")
+        quantize_people(0)
+        permute(0, 1)
+        permute(1, 0)
+        permute(1, 1)
+
+        x_tiles = {}
+        v_tiles = {}
+        v_codes = {}
+        joints = {}
+
+        def shape(s, h, ts):
+            b, c = divmod(s, G)
+            if ts[0] == 0:
+                x_tiles[s, h] = work.tile([P, 4, NP], F32, name="x", tag="x", bufs=4, align_bytes=64)
+            x = x_tiles[s, h]
+            codes, scales = b_codes[b]
+            for t in ts:
+                bank = banks.tile([P, NP], F32, name="bank_s", tag="bank")
+                nc.tensor.matmul_mx(
+                    out=bank[:],
+                    lhsT=s_words[c][h][:, 256 * t : 256 * (t + 1)].bitcast(FP4X4),
+                    lhsT_scale=s_scales[c][h][:, P * t : P * (t + 1)],
+                    rhs=codes[:].bitcast(FP8X4),
+                    rhs_scale=scales[:],
+                    start=True,
+                    stop=True,
+                )
+                nc.scalar.activation(
+                    out=x[:, t, :], in_=bank[:], func=IDENTITY, bias=mean[:, 2 * c + h, t : t + 1]
+                )
+
+        def scale_rows(eng, s, h, n0, n1, size):
+            x = x_tiles[s, h][:, :, n0:n1].rearrange("p t (c i) -> p c t i", i=4)
+            dst = v_tiles[s][:, h * 2048 + 4 * n0 : h * 2048 + 4 * n1].rearrange("p (c i t) -> p c t i", i=4, t=4)
+            fac = size[:, n0:n1].rearrange("p (c i) -> p c i", i=4).unsqueeze(2).to_broadcast([P, (n1 - n0) // 4, 4, 4])
+            eng.tensor_tensor(out=dst, in0=x, in1=fac, op=MULT)
+
+        def quantize_verts(s):
+            codes = work.tile([P, 2 * NP], U32, name="v_codes", tag="v_codes", bufs=2, align_bytes=64)
+            scales = work.tile([P, 2 * NP], U8, name="v_scales", tag="v_scales", bufs=2, align_bytes=64)
+            nc.vector.quantize_mx(out=codes[:].bitcast(FP8X4), scales=scales[:], in_=v_tiles[s][:])
+            v_codes[s] = (codes, scales)
+
+        def regress(s):
+            c = s % G
+            codes, scales = v_codes[s]
+            bank = joint_banks.tile([P, 4, J], F32, name="joint_bank")
+            joints[s] = bank
+            for i in range(4):
+                for h in range(2):
+                    cols = slice(h * NP + i * P, h * NP + (i + 1) * P)
+                    nc.tensor.matmul_mx(
+                        out=bank[:, i, :],
+                        lhsT=codes[:, cols].bitcast(FP8X4),
+                        lhsT_scale=scales[:, cols],
+                        rhs=r_words[:, 2 * c + h, :].bitcast(FP4X4),
+                        rhs_scale=r_scales[:, 2 * c + h, :],
+                        start=(h == 0),
+                        stop=(h == 1),
+                    )
+
+        def finish(s):
+            b, c = divmod(s, G)
+            res = work.tile([P, 4, J], F32, name="res", tag="res", bufs=3)
+            nc.vector.tensor_tensor(
+                out=res[:],
+                in0=joints[s][:],
+                in1=shift[:, b, c : 4 * G : G].unsqueeze(2).to_broadcast([P, 4, J]),
+                op=ADD,
+            )
+            nc.sync.dma_start(out=out_hbm[c, b], in_=res[:])
+
+        for s in range(STEPS + 2):
+            b, c = divmod(s, G)
+            if s < STEPS:
+                shape(s, 0, (0, 1, 2, 3))
+                shape(s, 1, (0,))
+            if 0 <= s - 2:
+                regress(s - 2)
+            if s < STEPS:
+                shape(s, 1, (1, 2, 3))
+            if 0 <= s - 2:
+                finish(s - 2)
+            if s == 1:
+                permute(2, 0)
+                permute(2, 1)
+            if c == 1 and b + 1 < BLOCKS:
+                spread_sizes(b + 1)
+                turn_people(b + 1, "ss")
+            if c == 2 and b + 1 < BLOCKS:
+                quantize_people(b + 1)
+            if s < STEPS:
+                v_tiles[s] = work.tile([P, 2 * 4 * NP], BF16, name="verts", tag="verts", bufs=3, align_bytes=64)
+                scale_rows(nc.vector, s, 0, 0, NP, size_ps[:, b % 2, :])
+            if 0 <= s - 1 < STEPS:
+                quantize_verts(s - 1)
+            if s < STEPS:
+                scale_rows(nc.vector, s, 1, 0, V_PERSONS, size_ps[:, b % 2, :])
+                for n0 in range(V_PERSONS, NP, G_CHUNK):
+                    scale_rows(nc.gpsimd, s, 1, n0, n0 + G_CHUNK, size_sb[b])

@@ -19,9 +19,15 @@ FLOPS = 2 * G * M * V * (K + J)
 P = 128
 NP = 512
 BLOCKS = M // NP
-STEPS = BLOCKS * G
-V_PERSONS = 128
+PLAN = (
+    [(0, 0, 0, 256), (0, 0, 256, 256), (0, 1, 0, 512), (0, 2, 0, 512)]
+    + [(b, c, 0, 512) for b in (1, 2) for c in range(G)]
+    + [(3, 0, 0, 512), (3, 1, 0, 512), (3, 2, 0, 256), (3, 2, 256, 256)]
+)
+STEPS = len(PLAN)
+G_PERSONS = [0, 0] + [256] * 10 + [64, 64]
 G_CHUNK = 128
+JOINTS_ON_SCALAR = (4, 8, 11, 12, 13)
 
 
 def tile_body_model_joints_s14_kernel(
@@ -39,7 +45,7 @@ def tile_body_model_joints_s14_kernel(
         ident_f32 = keep.tile([P, P], F32, name="ident_f32")
         ident_bf = keep.tile([P, P], BF16, name="ident_bf")
         raw_words = [keep.tile([P, 2 * V], U8, name="raw_words%d" % c, align_bytes=64) for c in range(G)]
-        raw_scales = [keep.tile([P, V], U8, name="raw_scales%d" % c, align_bytes=64) for c in range(G)]
+        raw_scales = keep.tile([P, G * V], U8, name="raw_scales", align_bytes=64)
         s_words = [[keep.tile([P, V], U8, name="s_words%d%d" % (c, h), align_bytes=64) for h in range(2)] for c in range(G)]
         s_scales = [[keep.tile([P, V // 2], U8, name="s_scales%d%d" % (c, h), align_bytes=64) for h in range(2)] for c in range(G)]
         r_words = keep.tile([P, 2 * G, 2 * J], U8, name="r_words", align_bytes=64)
@@ -54,51 +60,62 @@ def tile_body_model_joints_s14_kernel(
 
         people_hbm = betas.rearrange("(b p i) k -> b p i k", p=P, i=4)
         words_hbm = shape_words.bitcast(I32)
-        scales_hbm = shape_scales.bitcast(I32).rearrange("c (q r) n -> c r q n", r=4)
+        scales_hbm = shape_scales.bitcast(I32).rearrange("c (q r) n -> r q c n", r=4)
         rwords_hbm = reg_words.bitcast(I32).rearrange("g p n -> p g n")
         rscales_hbm = reg_scales.bitcast(I32).rearrange("g (q r) n -> r q g n", r=4)
         mean_hbm = template.rearrange("c n -> (c n)").rearrange("(g p t) -> p g t", p=P, t=4)
         out_hbm = out.rearrange("c (b p i) j -> c b p i j", p=P, i=4)
 
-        for c in range(G):
-            nc.vector.memset(raw_scales[c][:].bitcast(I32), 0)
-        nc.vector.memset(r_scales[:].rearrange("p g n -> p (g n)").bitcast(I32), 0)
         nc.vector.memset(dummy[:], 0.0)
+        nc.vector.memset(raw_scales[:].bitcast(I32), 0)
+        nc.vector.memset(r_scales[:].rearrange("p g n -> p (g n)").bitcast(I32), 0)
         make_identity(nc, ident_f32[:])
         make_identity(nc, ident_bf[:])
 
-        def load_words(c, h):
+        def load_people(b, i0, i1):
+            nc.sync.dma_start(out=people[b][:, i0:i1, :], in_=people_hbm[b, :, i0:i1, :])
+
+        def load_words(c, h0, h1):
             nc.sync.dma_start(
-                out=raw_words[c][:, h * V : (h + 1) * V].bitcast(I32), in_=words_hbm[c, :, h * 256 : (h + 1) * 256]
+                out=raw_words[c][:, h0 * V : h1 * V].bitcast(I32), in_=words_hbm[c, :, h0 * 256 : h1 * 256]
             )
 
-        def load_scales(eng, c):
-            for r in range(4):
-                eng.dma_start(out=raw_scales[c][:].bitcast(I32)[r:P:32, :], in_=scales_hbm[c, r])
-
-        load_words(0, 0)
-        load_scales(nc.sync, 0)
-        for i in (0, 2):
-            nc.sync.dma_start(out=people[0][:, i : i + 2, :], in_=people_hbm[0, :, i : i + 2, :])
-        load_words(0, 1)
-        for c in (1, 2):
-            for h in range(2):
-                load_words(c, h)
-        nc.sync.dma_start(out=r_words[:].rearrange("p g n -> p (g n)").bitcast(I32).rearrange("p (g n) -> p g n", g=2 * G), in_=rwords_hbm)
-        for b in range(1, BLOCKS):
-            nc.sync.dma_start(out=people[b][:], in_=people_hbm[b])
-
-        nc.scalar.dma_start(out=stat[:], in_=stature.rearrange("(b p i) -> p b i", p=P, i=4))
-        nc.scalar.dma_start(out=mean_bf[:], in_=mean_hbm)
-        nc.scalar.activation(out=dummy[:], in_=dummy[:], func=IDENTITY)
-        load_scales(nc.scalar, 1)
-        load_scales(nc.scalar, 2)
+        load_people(0, 0, 2)
+        load_people(0, 2, 4)
+        load_words(0, 0, 1)
         for r in range(4):
-            nc.scalar.dma_start(
+            nc.sync.dma_start(
+                out=raw_scales[:].bitcast(I32)[r:P:32, :].rearrange("p (c n) -> p c n", c=G), in_=scales_hbm[r]
+            )
+        load_words(0, 1, 2)
+        load_words(1, 0, 2)
+        for r in range(4):
+            nc.sync.dma_start(
                 out=r_scales[:].rearrange("p g n -> p (g n)").bitcast(I32)[r:P:32, :].rearrange("p (g n) -> p g n", g=2 * G),
                 in_=rscales_hbm[r],
             )
-        nc.scalar.dma_start(out=shift[:], in_=trans.rearrange("(b p i) c -> p b (i c)", p=P, i=4))
+        nc.sync.dma_start(
+            out=r_words[:].rearrange("p g n -> p (g n)").bitcast(I32).rearrange("p (g n) -> p g n", g=2 * G), in_=rwords_hbm
+        )
+        nc.sync.dma_start(out=shift[:], in_=trans.rearrange("(b p i) c -> p b (i c)", p=P, i=4))
+        load_words(2, 0, 2)
+        for b in range(1, BLOCKS):
+            load_people(b, 0, 4)
+        nc.scalar.dma_start(out=stat[:], in_=stature.rearrange("(b p i) -> p b i", p=P, i=4))
+        nc.scalar.dma_start(out=mean_bf[:], in_=mean_hbm)
+        nc.scalar.activation(out=dummy[:], in_=dummy[:], func=IDENTITY)
+
+        def permute_on_gpsimd(c, h):
+            for k in range(4):
+                m = slice(32 * k, 32 * (k + 1))
+                nc.gpsimd.tensor_copy(
+                    out=s_words[c][h][:].rearrange("p (t m b) -> p t m b", t=4, b=2)[:, :, m, :],
+                    in_=raw_words[c][:, h * V : (h + 1) * V].rearrange("p (m t b) -> p t m b", t=4, b=2)[:, :, m, :],
+                )
+            nc.gpsimd.tensor_copy(
+                out=s_scales[c][h][:].rearrange("p (t m) -> p t m", t=4),
+                in_=raw_scales[:, c * V + h * 512 : c * V + (h + 1) * 512].rearrange("p (m t) -> p t m", t=4),
+            )
 
         def permute(c, h):
             nc.vector.tensor_copy(
@@ -107,7 +124,7 @@ def tile_body_model_joints_s14_kernel(
             )
             nc.vector.tensor_copy(
                 out=s_scales[c][h][:].rearrange("p (t m) -> p t m", t=4),
-                in_=raw_scales[c][:, h * 512 : (h + 1) * 512].rearrange("p (m t) -> p t m", t=4),
+                in_=raw_scales[:, c * V + h * 512 : c * V + (h + 1) * 512].rearrange("p (m t) -> p t m", t=4),
             )
 
         b_codes = {}
@@ -122,84 +139,81 @@ def tile_body_model_joints_s14_kernel(
             nc.scalar.copy(out=sb[:], in_=half)
             size_sb[b] = sb
 
-        def turn_people(b, engines):
+        def turn_people(b, pair, eng):
             words = people[b][:].rearrange("p i k -> p (i k)").bitcast(F32)
-            gr = work.tile([P, NP * 4], BF16, name="b_grouped", tag="b_grouped", bufs=2, align_bytes=64)
-            grouped[b] = gr
-            for pair in range(2):
-                bank = banks.tile([P, 2, 2, P], F32, name="bank_t", tag="bank")
-                for a in range(2):
-                    i = 2 * pair + a
-                    for u in range(2):
-                        nc.tensor.transpose(bank[:, a, u, :], words[:, 256 * i + u : 256 * (i + 1) : 2], ident_f32[:])
-                dst = gr[:, pair * 1024 : (pair + 1) * 1024].bitcast(F32).rearrange("p (a n u) -> p a n u", a=2, u=2)
-                src = bank[:].rearrange("p a u n -> p a n u")
-                if engines[pair] == "v":
-                    nc.vector.tensor_copy(out=dst, in_=src)
-                else:
-                    nc.scalar.copy(out=dst, in_=src)
+            if pair == 0:
+                grouped[b] = work.tile([P, NP * 4], BF16, name="b_grouped", tag="b_grouped", bufs=2, align_bytes=64)
+            bank = banks.tile([P, 2, 2, P], F32, name="bank_t", tag="bank")
+            for a in range(2):
+                i = 2 * pair + a
+                for u in range(2):
+                    nc.tensor.transpose(bank[:, a, u, :], words[:, 256 * i + u : 256 * (i + 1) : 2], ident_f32[:])
+            dst = grouped[b][:, pair * 1024 : (pair + 1) * 1024].bitcast(F32).rearrange("p (a n u) -> p a n u", a=2, u=2)
+            src = bank[:].rearrange("p a u n -> p a n u")
+            if eng == "v":
+                nc.vector.tensor_copy(out=dst, in_=src)
+            else:
+                nc.scalar.copy(out=dst, in_=src)
 
-        def quantize_people(b):
-            codes = work.tile([P, NP], U32, name="b_codes", tag="b_codes", bufs=2, align_bytes=64)
-            scales = work.tile([P, NP], U8, name="b_scales", tag="b_scales", bufs=2, align_bytes=64)
-            nc.vector.quantize_mx(out=codes[:].bitcast(FP8X4), scales=scales[:], in_=grouped[b][:])
-            b_codes[b] = (codes, scales)
-
-        nc.vector.tensor_copy(out=mean[:], in_=mean_bf[:])
-        permute(0, 0)
-        spread_sizes(0)
-        turn_people(0, "sv")
-        quantize_people(0)
-        permute(0, 1)
-        permute(1, 0)
-        permute(1, 1)
+        def quantize_people(b, n0, n1):
+            if n0 == 0:
+                codes = work.tile([P, NP], U32, name="b_codes", tag="b_codes", bufs=2, align_bytes=64)
+                scales = work.tile([P, NP], U8, name="b_scales", tag="b_scales", bufs=2, align_bytes=64)
+                b_codes[b] = (codes, scales)
+            codes, scales = b_codes[b]
+            nc.vector.quantize_mx(out=codes[:, n0:n1].bitcast(FP8X4), scales=scales[:, n0:n1], in_=grouped[b][:, 4 * n0 : 4 * n1])
 
         x_tiles = {}
         v_tiles = {}
         v_codes = {}
         joints = {}
 
-        def shape(s, h, ts):
-            b, c = divmod(s, G)
+        def shape(s, h, ts, on_vector=()):
+            b, c, n0, n = PLAN[s]
             if ts[0] == 0:
-                x_tiles[s, h] = work.tile([P, 4, NP], F32, name="x", tag="x", bufs=4, align_bytes=64)
+                x_tiles[s, h] = work.tile([P, 4, NP], F32, name="x", tag="x", bufs=5, align_bytes=64)
             x = x_tiles[s, h]
             codes, scales = b_codes[b]
             for t in ts:
                 bank = banks.tile([P, NP], F32, name="bank_s", tag="bank")
                 nc.tensor.matmul_mx(
-                    out=bank[:],
+                    out=bank[:, :n],
                     lhsT=s_words[c][h][:, 256 * t : 256 * (t + 1)].bitcast(FP4X4),
                     lhsT_scale=s_scales[c][h][:, P * t : P * (t + 1)],
-                    rhs=codes[:].bitcast(FP8X4),
-                    rhs_scale=scales[:],
+                    rhs=codes[:, n0 : n0 + n].bitcast(FP8X4),
+                    rhs_scale=scales[:, n0 : n0 + n],
                     start=True,
                     stop=True,
                 )
-                nc.scalar.activation(
-                    out=x[:, t, :], in_=bank[:], func=IDENTITY, bias=mean[:, 2 * c + h, t : t + 1]
-                )
+                mean_t = mean[:, 2 * c + h, t : t + 1]
+                if t in on_vector:
+                    nc.vector.tensor_scalar(out=x[:, t, :n], in0=bank[:, :n], scalar1=mean_t, scalar2=None, op0=ADD)
+                else:
+                    nc.scalar.activation(out=x[:, t, :n], in_=bank[:, :n], func=IDENTITY, bias=mean_t)
 
-        def scale_rows(eng, s, h, n0, n1, size):
-            x = x_tiles[s, h][:, :, n0:n1].rearrange("p t (c i) -> p c t i", i=4)
-            dst = v_tiles[s][:, h * 2048 + 4 * n0 : h * 2048 + 4 * n1].rearrange("p (c i t) -> p c t i", i=4, t=4)
-            fac = size[:, n0:n1].rearrange("p (c i) -> p c i", i=4).unsqueeze(2).to_broadcast([P, (n1 - n0) // 4, 4, 4])
+        def scale_rows(eng, s, h, m0, m1):
+            b, c, n0, n = PLAN[s]
+            size = size_sb[b][:, :] if eng is nc.gpsimd else size_ps[:, b % 2, :]
+            x = x_tiles[s, h][:, :, m0:m1].rearrange("p t (c i) -> p c t i", i=4)
+            dst = v_tiles[s][:, 4 * (h * n + m0) : 4 * (h * n + m1)].rearrange("p (c i t) -> p c t i", i=4, t=4)
+            fac = size[:, n0 + m0 : n0 + m1].rearrange("p (c i) -> p c i", i=4).unsqueeze(2).to_broadcast([P, (m1 - m0) // 4, 4, 4])
             eng.tensor_tensor(out=dst, in0=x, in1=fac, op=MULT)
 
         def quantize_verts(s):
+            n = PLAN[s][3]
             codes = work.tile([P, 2 * NP], U32, name="v_codes", tag="v_codes", bufs=2, align_bytes=64)
             scales = work.tile([P, 2 * NP], U8, name="v_scales", tag="v_scales", bufs=2, align_bytes=64)
-            nc.vector.quantize_mx(out=codes[:].bitcast(FP8X4), scales=scales[:], in_=v_tiles[s][:])
+            nc.vector.quantize_mx(out=codes[:, : 2 * n].bitcast(FP8X4), scales=scales[:, : 2 * n], in_=v_tiles[s][:, : 8 * n])
             v_codes[s] = (codes, scales)
 
         def regress(s):
-            c = s % G
+            b, c, n0, n = PLAN[s]
             codes, scales = v_codes[s]
             bank = joint_banks.tile([P, 4, J], F32, name="joint_bank")
             joints[s] = bank
-            for i in range(4):
+            for i in range(n // P):
                 for h in range(2):
-                    cols = slice(h * NP + i * P, h * NP + (i + 1) * P)
+                    cols = slice(h * n + i * P, h * n + (i + 1) * P)
                     nc.tensor.matmul_mx(
                         out=bank[:, i, :],
                         lhsT=codes[:, cols].bitcast(FP8X4),
@@ -211,41 +225,62 @@ def tile_body_model_joints_s14_kernel(
                     )
 
         def finish(s):
-            b, c = divmod(s, G)
+            b, c, n0, n = PLAN[s]
+            i0, i1 = n0 // P, (n0 + n) // P
             res = work.tile([P, 4, J], F32, name="res", tag="res", bufs=3)
-            nc.vector.tensor_tensor(
-                out=res[:],
-                in0=joints[s][:],
-                in1=shift[:, b, c : 4 * G : G].unsqueeze(2).to_broadcast([P, 4, J]),
-                op=ADD,
-            )
-            nc.sync.dma_start(out=out_hbm[c, b], in_=res[:])
+            if s in JOINTS_ON_SCALAR:
+                for i in range(i1 - i0):
+                    k = G * (i0 + i) + c
+                    nc.scalar.activation(out=res[:, i, :], in_=joints[s][:, i, :], func=IDENTITY, bias=shift[:, b, k : k + 1])
+            else:
+                nc.vector.tensor_tensor(
+                    out=res[:, : i1 - i0, :],
+                    in0=joints[s][:, : i1 - i0, :],
+                    in1=shift[:, b, G * i0 + c : G * i1 : G].unsqueeze(2).to_broadcast([P, i1 - i0, J]),
+                    op=ADD,
+                )
+            nc.sync.dma_start(out=out_hbm[c, b, :, i0:i1, :], in_=res[:, : i1 - i0, :])
+
+        nc.vector.tensor_copy(out=mean[:], in_=mean_bf[:])
+        permute(0, 0)
+        spread_sizes(0)
+        turn_people(0, 0, "s")
+        quantize_people(0, 0, 256)
+        turn_people(0, 1, "s")
+        quantize_people(0, 256, 512)
+        permute(0, 1)
 
         for s in range(STEPS + 2):
-            b, c = divmod(s, G)
+            b, c, n0, n = PLAN[s] if s < STEPS else (0, 0, 0, 0)
+            late = s >= STEPS - 2
             if s < STEPS:
-                shape(s, 0, (0, 1, 2, 3))
-                shape(s, 1, (0,))
+                shape(s, 0, (0, 1, 2, 3), (2, 3) if s == 0 else ())
+                if late:
+                    shape(s, 1, (0, 1, 2, 3))
             if 0 <= s - 2:
                 regress(s - 2)
-            if s < STEPS:
-                shape(s, 1, (1, 2, 3))
+            if s < STEPS and not late:
+                shape(s, 1, (0, 1, 2, 3))
             if 0 <= s - 2:
                 finish(s - 2)
+            if s == 0:
+                permute(1, 0)
+                for h in range(2):
+                    permute_on_gpsimd(2, h)
             if s == 1:
-                permute(2, 0)
-                permute(2, 1)
+                permute(1, 1)
             if c == 1 and b + 1 < BLOCKS:
                 spread_sizes(b + 1)
-                turn_people(b + 1, "ss")
+                turn_people(b + 1, 0, "s")
+                turn_people(b + 1, 1, "s")
             if c == 2 and b + 1 < BLOCKS:
-                quantize_people(b + 1)
-            if s < STEPS:
-                v_tiles[s] = work.tile([P, 2 * 4 * NP], BF16, name="verts", tag="verts", bufs=3, align_bytes=64)
-                scale_rows(nc.vector, s, 0, 0, NP, size_ps[:, b % 2, :])
+                quantize_people(b + 1, 0, NP)
             if 0 <= s - 1 < STEPS:
                 quantize_verts(s - 1)
             if s < STEPS:
-                scale_rows(nc.vector, s, 1, 0, V_PERSONS, size_ps[:, b % 2, :])
-                for n0 in range(V_PERSONS, NP, G_CHUNK):
-                    scale_rows(nc.gpsimd, s, 1, n0, n0 + G_CHUNK, size_sb[b])
+                v_tiles[s] = work.tile([P, 2 * 4 * NP], BF16, name="verts", tag="verts", bufs=3, align_bytes=64)
+                g0 = n - G_PERSONS[s]
+                scale_rows(nc.vector, s, 0, 0, n)
+                scale_rows(nc.vector, s, 1, 0, g0)
+                for m0 in range(g0, n, G_CHUNK):
+                    scale_rows(nc.gpsimd, s, 1, m0, min(n, m0 + G_CHUNK))

@@ -19,15 +19,14 @@ FLOPS = 2 * G * M * V * (K + J)
 P = 128
 NP = 512
 BLOCKS = M // NP
-PLAN = (
-    [(0, 0, 0, 256), (0, 0, 256, 256), (0, 1, 0, 512), (0, 2, 0, 512)]
-    + [(b, c, 0, 512) for b in (1, 2) for c in range(G)]
-    + [(3, 0, 0, 512), (3, 1, 0, 512), (3, 2, 0, 256), (3, 2, 256, 256)]
-)
+PLAN = ((0, 0, 0, 256), (0, 0, 256, 256), (0, 1, 0, 512), (0, 2, 0, 512), (1, 0, 0, 512), (1, 1, 0, 512), (1, 2, 0, 512), (2, 0, 0, 512), (2, 1, 0, 512), (2, 2, 0, 512), (3, 0, 0, 512), (3, 1, 0, 512), (3, 2, 0, 256), (3, 2, 256, 256))
 STEPS = len(PLAN)
-G_PERSONS = [0, 0] + [256] * 10 + [64, 64]
-G_CHUNK = 128
-JOINTS_ON_SCALAR = (4, 8, 11, 12, 13)
+G_PERSONS = (0, 0, 192, 192, 240, 240, 240, 240, 240, 224, 224, 224, 96, 96)
+JOINTS_ON_SCALAR = (8, 9, 10, 11, 12, 13)
+ORDER = ("QAB", "QAB", "QAB", "QAB", "QAB", "QAB", "QAB", "QAB", "QAB", "QAB", "QAB", "QAB", "QAB", "QAB")
+LATE = (0, 0, 0, 0, 0, 0, 0, 0, 0, 0, 0, 0, 1, 1)
+X_BUFS = 5
+PERMUTE_ON_GPSIMD = ((2, 0), (2, 1))
 
 
 def tile_body_model_joints_s14_kernel(
@@ -50,8 +49,7 @@ def tile_body_model_joints_s14_kernel(
         s_scales = [[keep.tile([P, V // 2], U8, name="s_scales%d%d" % (c, h), align_bytes=64) for h in range(2)] for c in range(G)]
         r_words = keep.tile([P, 2 * G, 2 * J], U8, name="r_words", align_bytes=64)
         r_scales = keep.tile([P, 2 * G, J], U8, name="r_scales", align_bytes=64)
-        mean_bf = keep.tile([P, 2 * G, 4], BF16, name="mean_bf")
-        mean = keep.tile([P, 2 * G, 4], F32, name="mean")
+        mean = keep.tile([P, 2 * G, 4], BF16, name="mean")
         stat = keep.tile([P, BLOCKS, 4], BF16, name="stat")
         shift = keep.tile([P, BLOCKS, 4 * G], BF16, name="shift")
         dummy = keep.tile([P, 1], F32, name="dummy")
@@ -102,7 +100,7 @@ def tile_body_model_joints_s14_kernel(
         for b in range(1, BLOCKS):
             load_people(b, 0, 4)
         nc.scalar.dma_start(out=stat[:], in_=stature.rearrange("(b p i) -> p b i", p=P, i=4))
-        nc.scalar.dma_start(out=mean_bf[:], in_=mean_hbm)
+        nc.scalar.dma_start(out=mean[:], in_=mean_hbm)
         nc.scalar.activation(out=dummy[:], in_=dummy[:], func=IDENTITY)
 
         def permute_on_gpsimd(c, h):
@@ -135,9 +133,8 @@ def tile_body_model_joints_s14_kernel(
             half = size_ps[:, b % 2, :]
             for i in range(4):
                 nc.tensor.transpose(half[:, i * P : (i + 1) * P], stat[:, b, i : i + 1].to_broadcast([P, P]), ident_bf[:])
-            sb = work.tile([P, NP], BF16, name="size_sb", tag="size_sb", bufs=2)
-            nc.scalar.copy(out=sb[:], in_=half)
-            size_sb[b] = sb
+            size_sb[b] = work.tile([P, NP], BF16, name="size_sb", tag="size_sb", bufs=2)
+            nc.scalar.copy(out=size_sb[b][:], in_=half)
 
         def turn_people(b, pair, eng):
             words = people[b][:].rearrange("p i k -> p (i k)").bitcast(F32)
@@ -171,7 +168,7 @@ def tile_body_model_joints_s14_kernel(
         def shape(s, h, ts, on_vector=()):
             b, c, n0, n = PLAN[s]
             if ts[0] == 0:
-                x_tiles[s, h] = work.tile([P, 4, NP], F32, name="x", tag="x", bufs=5, align_bytes=64)
+                x_tiles[s, h] = work.tile([P, 4, NP], F32, name="x", tag="x", bufs=X_BUFS, align_bytes=64)
             x = x_tiles[s, h]
             codes, scales = b_codes[b]
             for t in ts:
@@ -192,10 +189,12 @@ def tile_body_model_joints_s14_kernel(
                     nc.scalar.activation(out=x[:, t, :n], in_=bank[:, :n], func=IDENTITY, bias=mean_t)
 
         def scale_rows(eng, s, h, m0, m1):
+            if m0 == m1:
+                return
             b, c, n0, n = PLAN[s]
-            size = size_sb[b][:, :] if eng is nc.gpsimd else size_ps[:, b % 2, :]
+            size = size_sb[b][:] if eng is nc.gpsimd else size_ps[:, b % 2, :]
             x = x_tiles[s, h][:, :, m0:m1].rearrange("p t (c i) -> p c t i", i=4)
-            dst = v_tiles[s][:, 4 * (h * n + m0) : 4 * (h * n + m1)].rearrange("p (c i t) -> p c t i", i=4, t=4)
+            dst = v_tiles[s, h][:, 4 * m0 : 4 * m1].rearrange("p (c i t) -> p c t i", i=4, t=4)
             fac = size[:, n0 + m0 : n0 + m1].rearrange("p (c i) -> p c i", i=4).unsqueeze(2).to_broadcast([P, (m1 - m0) // 4, 4, 4])
             eng.tensor_tensor(out=dst, in0=x, in1=fac, op=MULT)
 
@@ -203,7 +202,12 @@ def tile_body_model_joints_s14_kernel(
             n = PLAN[s][3]
             codes = work.tile([P, 2 * NP], U32, name="v_codes", tag="v_codes", bufs=2, align_bytes=64)
             scales = work.tile([P, 2 * NP], U8, name="v_scales", tag="v_scales", bufs=2, align_bytes=64)
-            nc.vector.quantize_mx(out=codes[:, : 2 * n].bitcast(FP8X4), scales=scales[:, : 2 * n], in_=v_tiles[s][:, : 8 * n])
+            for h in range(2):
+                nc.vector.quantize_mx(
+                    out=codes[:, h * n : (h + 1) * n].bitcast(FP8X4),
+                    scales=scales[:, h * n : (h + 1) * n],
+                    in_=v_tiles[s, h][:, : 4 * n],
+                )
             v_codes[s] = (codes, scales)
 
         def regress(s):
@@ -241,7 +245,6 @@ def tile_body_model_joints_s14_kernel(
                 )
             nc.sync.dma_start(out=out_hbm[c, b, :, i0:i1, :], in_=res[:, : i1 - i0, :])
 
-        nc.vector.tensor_copy(out=mean[:], in_=mean_bf[:])
         permute(0, 0)
         spread_sizes(0)
         turn_people(0, 0, "s")
@@ -252,7 +255,8 @@ def tile_body_model_joints_s14_kernel(
 
         for s in range(STEPS + 2):
             b, c, n0, n = PLAN[s] if s < STEPS else (0, 0, 0, 0)
-            late = s >= STEPS - 2
+            order = ORDER[s] if s < STEPS else "Q"
+            late = s < STEPS and LATE[s]
             if s < STEPS:
                 shape(s, 0, (0, 1, 2, 3), (2, 3) if s == 0 else ())
                 if late:
@@ -261,26 +265,32 @@ def tile_body_model_joints_s14_kernel(
                 regress(s - 2)
             if s < STEPS and not late:
                 shape(s, 1, (0, 1, 2, 3))
-            if 0 <= s - 2:
+            if 0 <= s - 2 and "O" not in order:
                 finish(s - 2)
+            if s < 2:
+                if (1, s) not in PERMUTE_ON_GPSIMD:
+                    permute(1, s)
             if s == 0:
-                permute(1, 0)
-                for h in range(2):
-                    permute_on_gpsimd(2, h)
-            if s == 1:
-                permute(1, 1)
+                for cc, h in PERMUTE_ON_GPSIMD:
+                    permute_on_gpsimd(cc, h)
             if c == 1 and b + 1 < BLOCKS:
                 spread_sizes(b + 1)
                 turn_people(b + 1, 0, "s")
                 turn_people(b + 1, 1, "s")
             if c == 2 and b + 1 < BLOCKS:
                 quantize_people(b + 1, 0, NP)
-            if 0 <= s - 1 < STEPS:
-                quantize_verts(s - 1)
-            if s < STEPS:
-                v_tiles[s] = work.tile([P, 2 * 4 * NP], BF16, name="verts", tag="verts", bufs=3, align_bytes=64)
-                g0 = n - G_PERSONS[s]
-                scale_rows(nc.vector, s, 0, 0, n)
-                scale_rows(nc.vector, s, 1, 0, g0)
-                for m0 in range(g0, n, G_CHUNK):
-                    scale_rows(nc.gpsimd, s, 1, m0, min(n, m0 + G_CHUNK))
+            for what in order:
+                if what == "O" and 0 <= s - 2:
+                    finish(s - 2)
+                if what == "Q" and 0 <= s - 1 < STEPS:
+                    quantize_verts(s - 1)
+                if what == "A":
+                    for h in range(2):
+                        v_tiles[s, h] = work.tile(
+                            [P, 4 * NP], BF16, name="verts%d" % h, tag="verts%d" % h, bufs=2 - h, align_bytes=64
+                        )
+                    scale_rows(nc.vector, s, 0, 0, n)
+                if what == "B":
+                    g0 = n - G_PERSONS[s]
+                    scale_rows(nc.vector, s, 1, 0, g0)
+                    scale_rows(nc.gpsimd, s, 1, g0, n)

from contextlib import ExitStack

import concourse.mybir as mybir
from concourse.masks import make_identity

F32 = mybir.dt.float32
BF16 = mybir.dt.bfloat16
I32 = mybir.dt.int32
U32 = mybir.dt.uint32
U8 = mybir.dt.uint8
FP8X4 = mybir.dt.float8_e4m3fn_x4
FP4X4 = mybir.dt.float4_e2m1fn_x4
ADD = mybir.AluOpType.add
MULT = mybir.AluOpType.mult
IDENTITY = mybir.ActivationFunctionType.Identity

G, M, K, V, J = 3, 2048, 512, 1024, 128
FLOPS = 2 * G * M * V * (K + J)
P = 128
NP = 512
BLOCKS = M // NP
PLAN = ((0, 0, 0, 256), (0, 0, 256, 256), (0, 1, 0, 512), (0, 2, 0, 512), (1, 0, 0, 512), (1, 1, 0, 512), (1, 2, 0, 512), (2, 0, 0, 512), (2, 1, 0, 512), (2, 2, 0, 512), (3, 0, 0, 512), (3, 1, 0, 512), (3, 2, 0, 256), (3, 2, 256, 256))
STEPS = len(PLAN)
G_PERSONS = (0, 0, 192, 192, 240, 240, 240, 240, 240, 224, 224, 224, 96, 96)
JOINTS_ON_SCALAR = (8, 9, 10, 11, 12, 13)
ORDER = ("QAB", "QAB", "QAB", "QAB", "QAB", "QAB", "QAB", "QAB", "QAB", "QAB", "QAB", "QAB", "QAB", "QAB")
LATE = (0, 0, 0, 0, 0, 0, 0, 0, 0, 0, 0, 0, 1, 1)
X_BUFS = 5
PERMUTE_ON_GPSIMD = ((2, 0), (2, 1))


def tile_body_model_joints_s14_kernel(
    tc, betas, shape_words, shape_scales, template, stature, reg_words, reg_scales, trans, out
):
    nc = tc.nc
    with ExitStack() as ctx:
        keep = ctx.enter_context(tc.tile_pool(name="keep", bufs=1))
        work = ctx.enter_context(tc.tile_pool(name="work", bufs=3))
        banks = ctx.enter_context(tc.psum_pool(name="banks", bufs=6))
        joint_banks = ctx.enter_context(tc.psum_pool(name="joint_banks", bufs=1))
        size_banks = ctx.enter_context(tc.psum_pool(name="size_banks", bufs=1))
        ctx.enter_context(tc.manual_schedule())

        ident_f32 = keep.tile([P, P], F32, name="ident_f32")
        ident_bf = keep.tile([P, P], BF16, name="ident_bf")
        raw_words = [keep.tile([P, 2 * V], U8, name="raw_words%d" % c, align_bytes=64) for c in range(G)]
        raw_scales = keep.tile([P, G * V], U8, name="raw_scales", align_bytes=64)
        s_words = [[keep.tile([P, V], U8, name="s_words%d%d" % (c, h), align_bytes=64) for h in range(2)] for c in range(G)]
        s_scales = [[keep.tile([P, V // 2], U8, name="s_scales%d%d" % (c, h), align_bytes=64) for h in range(2)] for c in range(G)]
        r_words = keep.tile([P, 2 * G, 2 * J], U8, name="r_words", align_bytes=64)
        r_scales = keep.tile([P, 2 * G, J], U8, name="r_scales", align_bytes=64)
        mean = keep.tile([P, 2 * G, 4], BF16, name="mean")
        stat = keep.tile([P, BLOCKS, 4], BF16, name="stat")
        shift = keep.tile([P, BLOCKS, 4 * G], BF16, name="shift")
        dummy = keep.tile([P, 1], F32, name="dummy")
        people = [keep.tile([P, 4, K], BF16, name="people%d" % b, align_bytes=64) for b in range(BLOCKS)]
        size_ps = size_banks.tile([P, 2, NP], BF16, name="size_ps")

        people_hbm = betas.rearrange("(b p i) k -> b p i k", p=P, i=4)
        words_hbm = shape_words.bitcast(I32)
        scales_hbm = shape_scales.bitcast(I32).rearrange("c (q r) n -> r q c n", r=4)
        rwords_hbm = reg_words.bitcast(I32).rearrange("g p n -> p g n")
        rscales_hbm = reg_scales.bitcast(I32).rearrange("g (q r) n -> r q g n", r=4)
        mean_hbm = template.rearrange("c n -> (c n)").rearrange("(g p t) -> p g t", p=P, t=4)
        out_hbm = out.rearrange("c (b p i) j -> c b p i j", p=P, i=4)

        nc.vector.memset(dummy[:], 0.0)
        nc.vector.memset(raw_scales[:].bitcast(I32), 0)
        nc.vector.memset(r_scales[:].rearrange("p g n -> p (g n)").bitcast(I32), 0)
        make_identity(nc, ident_f32[:])
        make_identity(nc, ident_bf[:])

        def load_people(b, i0, i1):
            nc.sync.dma_start(out=people[b][:, i0:i1, :], in_=people_hbm[b, :, i0:i1, :])

        def load_words(c, h0, h1):
            nc.sync.dma_start(
                out=raw_words[c][:, h0 * V : h1 * V].bitcast(I32), in_=words_hbm[c, :, h0 * 256 : h1 * 256]
            )

        load_people(0, 0, 2)
        load_people(0, 2, 4)
        load_words(0, 0, 1)
        for r in range(4):
            nc.sync.dma_start(
                out=raw_scales[:].bitcast(I32)[r:P:32, :].rearrange("p (c n) -> p c n", c=G), in_=scales_hbm[r]
            )
        load_words(0, 1, 2)
        load_words(1, 0, 2)
        for r in range(4):
            nc.sync.dma_start(
                out=r_scales[:].rearrange("p g n -> p (g n)").bitcast(I32)[r:P:32, :].rearrange("p (g n) -> p g n", g=2 * G),
                in_=rscales_hbm[r],
            )
        nc.sync.dma_start(
            out=r_words[:].rearrange("p g n -> p (g n)").bitcast(I32).rearrange("p (g n) -> p g n", g=2 * G), in_=rwords_hbm
        )
        nc.sync.dma_start(out=shift[:], in_=trans.rearrange("(b p i) c -> p b (i c)", p=P, i=4))
        load_words(2, 0, 2)
        for b in range(1, BLOCKS):
            load_people(b, 0, 4)
        nc.scalar.dma_start(out=stat[:], in_=stature.rearrange("(b p i) -> p b i", p=P, i=4))
        nc.scalar.dma_start(out=mean[:], in_=mean_hbm)
        nc.scalar.activation(out=dummy[:], in_=dummy[:], func=IDENTITY)

        def permute_on_gpsimd(c, h):
            for k in range(4):
                m = slice(32 * k, 32 * (k + 1))
                nc.gpsimd.tensor_copy(
                    out=s_words[c][h][:].rearrange("p (t m b) -> p t m b", t=4, b=2)[:, :, m, :],
                    in_=raw_words[c][:, h * V : (h + 1) * V].rearrange("p (m t b) -> p t m b", t=4, b=2)[:, :, m, :],
                )
            nc.gpsimd.tensor_copy(
                out=s_scales[c][h][:].rearrange("p (t m) -> p t m", t=4),
                in_=raw_scales[:, c * V + h * 512 : c * V + (h + 1) * 512].rearrange("p (m t) -> p t m", t=4),
            )

        def permute(c, h):
            nc.vector.tensor_copy(
                out=s_words[c][h][:].rearrange("p (t m b) -> p t m b", t=4, b=2),
                in_=raw_words[c][:, h * V : (h + 1) * V].rearrange("p (m t b) -> p t m b", t=4, b=2),
            )
            nc.vector.tensor_copy(
                out=s_scales[c][h][:].rearrange("p (t m) -> p t m", t=4),
                in_=raw_scales[:, c * V + h * 512 : c * V + (h + 1) * 512].rearrange("p (m t) -> p t m", t=4),
            )

        b_codes = {}
        size_sb = {}
        grouped = {}

        def spread_sizes(b):
            half = size_ps[:, b % 2, :]
            for i in range(4):
                nc.tensor.transpose(half[:, i * P : (i + 1) * P], stat[:, b, i : i + 1].to_broadcast([P, P]), ident_bf[:])
            size_sb[b] = work.tile([P, NP], BF16, name="size_sb", tag="size_sb", bufs=2)
            nc.scalar.copy(out=size_sb[b][:], in_=half)

        def turn_people(b, pair, eng):
            words = people[b][:].rearrange("p i k -> p (i k)").bitcast(F32)
            if pair == 0:
                grouped[b] = work.tile([P, NP * 4], BF16, name="b_grouped", tag="b_grouped", bufs=2, align_bytes=64)
            bank = banks.tile([P, 2, 2, P], F32, name="bank_t", tag="bank")
            for a in range(2):
                i = 2 * pair + a
                for u in range(2):
                    nc.tensor.transpose(bank[:, a, u, :], words[:, 256 * i + u : 256 * (i + 1) : 2], ident_f32[:])
            dst = grouped[b][:, pair * 1024 : (pair + 1) * 1024].bitcast(F32).rearrange("p (a n u) -> p a n u", a=2, u=2)
            src = bank[:].rearrange("p a u n -> p a n u")
            if eng == "v":
                nc.vector.tensor_copy(out=dst, in_=src)
            else:
                nc.scalar.copy(out=dst, in_=src)

        def quantize_people(b, n0, n1):
            if n0 == 0:
                codes = work.tile([P, NP], U32, name="b_codes", tag="b_codes", bufs=2, align_bytes=64)
                scales = work.tile([P, NP], U8, name="b_scales", tag="b_scales", bufs=2, align_bytes=64)
                b_codes[b] = (codes, scales)
            codes, scales = b_codes[b]
            nc.vector.quantize_mx(out=codes[:, n0:n1].bitcast(FP8X4), scales=scales[:, n0:n1], in_=grouped[b][:, 4 * n0 : 4 * n1])

        x_tiles = {}
        v_tiles = {}
        v_codes = {}
        joints = {}

        def shape(s, h, ts, on_vector=()):
            b, c, n0, n = PLAN[s]
            if ts[0] == 0:
                x_tiles[s, h] = work.tile([P, 4, NP], F32, name="x", tag="x", bufs=X_BUFS, align_bytes=64)
            x = x_tiles[s, h]
            codes, scales = b_codes[b]
            for t in ts:
                bank = banks.tile([P, NP], F32, name="bank_s", tag="bank")
                nc.tensor.matmul_mx(
                    out=bank[:, :n],
                    lhsT=s_words[c][h][:, 256 * t : 256 * (t + 1)].bitcast(FP4X4),
                    lhsT_scale=s_scales[c][h][:, P * t : P * (t + 1)],
                    rhs=codes[:, n0 : n0 + n].bitcast(FP8X4),
                    rhs_scale=scales[:, n0 : n0 + n],
                    start=True,
                    stop=True,
                )
                mean_t = mean[:, 2 * c + h, t : t + 1]
                if t in on_vector:
                    nc.vector.tensor_scalar(out=x[:, t, :n], in0=bank[:, :n], scalar1=mean_t, scalar2=None, op0=ADD)
                else:
                    nc.scalar.activation(out=x[:, t, :n], in_=bank[:, :n], func=IDENTITY, bias=mean_t)

        def scale_rows(eng, s, h, m0, m1):
            if m0 == m1:
                return
            b, c, n0, n = PLAN[s]
            size = size_sb[b][:] if eng is nc.gpsimd else size_ps[:, b % 2, :]
            x = x_tiles[s, h][:, :, m0:m1].rearrange("p t (c i) -> p c t i", i=4)
            dst = v_tiles[s, h][:, 4 * m0 : 4 * m1].rearrange("p (c i t) -> p c t i", i=4, t=4)
            fac = size[:, n0 + m0 : n0 + m1].rearrange("p (c i) -> p c i", i=4).unsqueeze(2).to_broadcast([P, (m1 - m0) // 4, 4, 4])
            eng.tensor_tensor(out=dst, in0=x, in1=fac, op=MULT)

        def quantize_verts(s):
            n = PLAN[s][3]
            codes = work.tile([P, 2 * NP], U32, name="v_codes", tag="v_codes", bufs=2, align_bytes=64)
            scales = work.tile([P, 2 * NP], U8, name="v_scales", tag="v_scales", bufs=2, align_bytes=64)
            for h in range(2):
                nc.vector.quantize_mx(
                    out=codes[:, h * n : (h + 1) * n].bitcast(FP8X4),
                    scales=scales[:, h * n : (h + 1) * n],
                    in_=v_tiles[s, h][:, : 4 * n],
                )
            v_codes[s] = (codes, scales)

        def regress(s):
            b, c, n0, n = PLAN[s]
            codes, scales = v_codes[s]
            bank = joint_banks.tile([P, 4, J], F32, name="joint_bank")
            joints[s] = bank
            for i in range(n // P):
                for h in range(2):
                    cols = slice(h * n + i * P, h * n + (i + 1) * P)
                    nc.tensor.matmul_mx(
                        out=bank[:, i, :],
                        lhsT=codes[:, cols].bitcast(FP8X4),
                        lhsT_scale=scales[:, cols],
                        rhs=r_words[:, 2 * c + h, :].bitcast(FP4X4),
                        rhs_scale=r_scales[:, 2 * c + h, :],
                        start=(h == 0),
                        stop=(h == 1),
                    )

        def finish(s):
            b, c, n0, n = PLAN[s]
            i0, i1 = n0 // P, (n0 + n) // P
            res = work.tile([P, 4, J], F32, name="res", tag="res", bufs=3)
            if s in JOINTS_ON_SCALAR:
                for i in range(i1 - i0):
                    k = G * (i0 + i) + c
                    nc.scalar.activation(out=res[:, i, :], in_=joints[s][:, i, :], func=IDENTITY, bias=shift[:, b, k : k + 1])
            else:
                nc.vector.tensor_tensor(
                    out=res[:, : i1 - i0, :],
                    in0=joints[s][:, : i1 - i0, :],
                    in1=shift[:, b, G * i0 + c : G * i1 : G].unsqueeze(2).to_broadcast([P, i1 - i0, J]),
                    op=ADD,
                )
            nc.sync.dma_start(out=out_hbm[c, b, :, i0:i1, :], in_=res[:, : i1 - i0, :])

        permute(0, 0)
        spread_sizes(0)
        turn_people(0, 0, "s")
        quantize_people(0, 0, 256)
        turn_people(0, 1, "s")
        quantize_people(0, 256, 512)
        permute(0, 1)

        for s in range(STEPS + 2):
            b, c, n0, n = PLAN[s] if s < STEPS else (0, 0, 0, 0)
            order = ORDER[s] if s < STEPS else "Q"
            late = s < STEPS and LATE[s]
            if s < STEPS:
                shape(s, 0, (0, 1, 2, 3), (2, 3) if s == 0 else ())
                if late:
                    shape(s, 1, (0, 1, 2, 3))
            if 0 <= s - 2:
                regress(s - 2)
            if s < STEPS and not late:
                shape(s, 1, (0, 1, 2, 3))
            if 0 <= s - 2 and "O" not in order:
                finish(s - 2)
            if s < 2:
                if (1, s) not in PERMUTE_ON_GPSIMD:
                    permute(1, s)
            if s == 0:
                for cc, h in PERMUTE_ON_GPSIMD:
                    permute_on_gpsimd(cc, h)
            if c == 1 and b + 1 < BLOCKS:
                spread_sizes(b + 1)
                turn_people(b + 1, 0, "s")
                turn_people(b + 1, 1, "s")
            if c == 2 and b + 1 < BLOCKS:
                quantize_people(b + 1, 0, NP)
            for what in order:
                if what == "O" and 0 <= s - 2:
                    finish(s - 2)
                if what == "Q" and 0 <= s - 1 < STEPS:
                    quantize_verts(s - 1)
                if what == "A":
                    for h in range(2):
                        v_tiles[s, h] = work.tile(
                            [P, 4 * NP], BF16, name="verts%d" % h, tag="verts%d" % h, bufs=2 - h, align_bytes=64
                        )
                    scale_rows(nc.vector, s, 0, 0, n)
                if what == "B":
                    g0 = n - G_PERSONS[s]
                    scale_rows(nc.vector, s, 1, 0, g0)
                    scale_rows(nc.gpsimd, s, 1, g0, n)
